import numpy as np
import ml_dtypes


def mxq(x, axis, fmt="e4m3"):
    dtype, down = {"e4m3": (ml_dtypes.float8_e4m3fn, 7), "e5m2": (ml_dtypes.float8_e5m2, 14)}[fmt]
    v = np.moveaxis(np.asarray(x, np.float32).astype(ml_dtypes.bfloat16).astype(np.float64), axis, -1)
    blocks = v.reshape(v.shape[:-1] + (-1, 32))
    amax = np.abs(blocks).max(-1, keepdims=True)
    byte = np.maximum(np.where(amax > 0, np.frexp(amax)[1] - 1 + 127, 0) - down, 1)
    scale = np.exp2(byte - 127.0)
    codes = (blocks / scale).astype(np.float32).astype(dtype).astype(np.float64)
    return np.moveaxis((codes * scale).reshape(v.shape), -1, axis)


WIDE = False


def mx_kscale(k):
    if not WIDE:
        return np.ones(k)
    levels = np.array([10, -10, 5, -5, 0])
    if k % 512:
        return np.exp2(np.random.permutation(np.resize(levels, k // 32))).repeat(32)
    a = np.empty((k // 512, 16))
    for p in range(k // 512):
        a[p, :8] = np.random.permutation(np.resize(levels, 8))
        for g in range(8):
            far = levels[np.abs(levels - a[p, g]) >= 10]
            a[p, g + 8] = far[np.random.randint(len(far))]
    return np.exp2(a.ravel()).repeat(32)


def f64(x):
    return np.asarray(x).astype(np.float64)


def striped(idx):
    return np.tile(idx.reshape(-1, 16).T, (8, 1)).astype(np.uint16)


def unstriped(offs):
    return offs[:16].T.reshape(-1).astype(np.int64)


def pack_weight(w):
    k, n = w.shape
    w = f64(np.asarray(w, np.float32).astype(ml_dtypes.bfloat16)).reshape(k // 32, 32, n)
    amax = np.abs(w).max(1)
    byte = np.clip(np.where(amax > 0, np.frexp(amax)[1] - 1 + 127 - 7, 1), 1, 254)
    scaled = (w * np.exp2(127.0 - byte)[:, None, :]).reshape(k, n).astype(np.float32)
    words = np.ascontiguousarray(scaled.reshape(k // 512, 128, 4, n).transpose(0, 1, 3, 2)).astype(ml_dtypes.float8_e4m3fn).view(np.uint8)
    return words, np.ascontiguousarray(byte.astype(np.uint8).reshape(k // 512, 16, n))


def unpack_weight(words, scales):
    g, p, n, _ = words.shape
    vals = np.ascontiguousarray(words).view(ml_dtypes.float8_e4m3fn).astype(np.float64) * np.repeat(np.exp2(scales.astype(np.float64) - 127.0), 8, axis=1)[..., None]
    return vals.transpose(0, 1, 3, 2).reshape(g * 512, n)


K, T, S, N, H, U = 512, 1024, 512, 256, 512, 1024


def setup_inputs():
    n = np.random.standard_normal
    s = mx_kscale(K)[:, None]
    u = mx_kscale(H)
    packed_xT = pack_weight(n((K, T)) * s)
    return {
        "x_words": packed_xT[0],
        "x_scales": packed_xT[1],
        "w1": (n((K, H)) / np.sqrt(K) / s).astype(np.float32),
        "unit": (np.random.uniform(0.6, 1.4, (H, 1)) * u[:, None]).astype(np.float32),
        "w2": (n((H, N)) / np.sqrt(H) / u[:, None]).astype(np.float32),
        "offs": striped(np.random.permutation(T)[:S]),
        "ga": striped(np.random.permutation(np.concatenate([np.arange(S), np.random.randint(0, S, U - S)]))),
        "gb": striped(np.random.permutation(np.concatenate([np.arange(S), np.random.randint(0, S, U - S)]))),
        "gc": striped(np.random.permutation(np.concatenate([np.arange(S), np.random.randint(0, S, U - S)]))),
    }


def reference(x_words, x_scales, w1, unit, w2, offs, ga, gb, gc):
    xq = unpack_weight(x_words, x_scales)[:, unstriped(offs)]
    y = mxq(f64(w1), 0, "e4m3").T @ xq
    ya = y[:, unstriped(ga)]
    yb_ = y[:, unstriped(gb)]
    ygc = y[:, unstriped(gc)]
    hid = f64(unit) * (ya * yb_ + ygc)
    return mxq(f64(w2), 0, "e4m3").T @ mxq(hid, 0, "e4m3")

@@ -1,0 +1,176 @@
+from contextlib import ExitStack
+
+import concourse.mybir as mybir
+
+K, T, S, N, H, U = 512, 1024, 512, 256, 512, 1024
+FLOPS = 2 * K * H * S + 2 * H * N * U
+
+F32 = mybir.dt.float32
+BF16 = mybir.dt.bfloat16
+I32 = mybir.dt.int32
+U32 = mybir.dt.uint32
+U16 = mybir.dt.uint16
+U8 = mybir.dt.uint8
+FP8X4 = mybir.dt.float8_e4m3fn_x4
+COPY = mybir.ActivationFunctionType.Copy
+MULT = mybir.AluOpType.mult
+ADD = mybir.AluOpType.add
+
+P = 128
+PACK = 4
+LIST_ROWS = 16
+CHUNKS = (256, 256, 256, 128, 128)
+
+
+def tile_picked_ytripco_add_p_kernel(tc, x_words, x_scales, w1, unit, w2, offs, ga, gb, gc, out):
+    nc = tc.nc
+    with ExitStack() as ctx:
+        keep = ctx.enter_context(tc.tile_pool(name="keep", bufs=1))
+        psum = ctx.enter_context(tc.psum_pool(name="psum", bufs=1))
+
+        x_word_table = keep.tile([P, T], U32, name="x_word_table")
+        x_scale_table = keep.tile([P, T], U8, name="x_scale_table")
+        offs_list = keep.tile([P, S // LIST_ROWS], U16, name="offs_list")
+        ga_list = keep.tile([P, U // LIST_ROWS], U16, name="ga_list")
+        gb_list = keep.tile([P, U // LIST_ROWS], U16, name="gb_list")
+        gc_list = keep.tile([P, U // LIST_ROWS], U16, name="gc_list")
+        w1_raw = [keep.tile([P, PACK, H // 2], F32, name=f"w1_raw{half}") for half in range(2)]
+        w2_raw = keep.tile([P, PACK, N], F32, name="w2_raw")
+        unit_cols = keep.tile([P, PACK], F32, name="unit_cols")
+
+        nc.vector.memset(x_scale_table[:].bitcast(I32), 0)
+        nc.sync.dma_start(x_word_table[:].bitcast(I32), x_words[0].rearrange("p c r -> p (c r)").bitcast(I32))
+        nc.sync.dma_start(offs_list[:], offs)
+        for quad in range(4):
+            nc.scalar.dma_start(
+                x_scale_table[32 * quad : 32 * quad + 4, :].bitcast(I32),
+                x_scales[0, 4 * quad : 4 * quad + 4, :].bitcast(I32),
+            )
+        w1_rows = w1.rearrange("(p j) c -> p j c", j=PACK)
+        for half in range(2):
+            nc.sync.dma_start(w1_raw[half][:], w1_rows[:, :, half * (H // 2) : (half + 1) * (H // 2)])
+        nc.sync.dma_start(gb_list[:], gb)
+        nc.sync.dma_start(unit_cols[:], unit.rearrange("(p t) o -> p (t o)", t=PACK))
+        nc.sync.dma_start(ga_list[:], ga)
+        nc.sync.dma_start(gc_list[:], gc)
+        nc.sync.dma_start(w2_raw[:], w2.rearrange("(p j) n -> p j n", j=PACK))
+
+        x_codes = keep.tile([P, S], U32, name="x_codes", align_bytes=64)
+        x_plane = keep.tile([P, S], U8, name="x_plane", align_bytes=64)
+        nc.vector.tensor_copy(x_codes[:], x_word_table[:].indirect(offs_list[:]))
+        nc.vector.tensor_copy(x_plane[:], x_scale_table[:].indirect(offs_list[:]))
+
+        y_plain = [keep.tile([P, S], F32, name=f"y_plain{t}") for t in range(PACK)]
+        y_unit = [keep.tile([P, S], F32, name=f"y_unit{t}") for t in range(PACK)]
+        for pair in range(2):
+            grouped = keep.tile([P, 2, P, PACK], BF16, name=f"w1_grouped{pair}", align_bytes=64)
+            for half in range(2):
+                dst = grouped[:, :, half * 64 : (half + 1) * 64, :].rearrange("p t m j -> p m j t")
+                src = w1_raw[half][:].rearrange("p j (m t) -> p m j t", t=PACK)[:, :, :, 2 * pair : 2 * pair + 2]
+                if half == 0:
+                    nc.scalar.activation(dst, src, COPY)
+                else:
+                    nc.vector.tensor_copy(dst, src)
+            codes = keep.tile([P, 2 * P], U32, name=f"w1_codes{pair}", align_bytes=64)
+            plane = keep.tile([P, 2 * P], U8, name=f"w1_plane{pair}", align_bytes=64)
+            nc.vector.quantize_mx(
+                out=codes[:].bitcast(FP8X4), scales=plane[:], in_=grouped[:].rearrange("p t m j -> p (t m j)")
+            )
+            for slot in range(2):
+                t = 2 * pair + slot
+                y_bank = psum.tile([P, S], F32, name=f"y_bank{t}")
+                nc.tensor.matmul_mx(
+                    out=y_bank[:],
+                    lhsT=codes[:, slot * P : (slot + 1) * P].bitcast(FP8X4),
+                    lhsT_scale=plane[:, slot * P : (slot + 1) * P],
+                    rhs=x_codes[:].bitcast(FP8X4),
+                    rhs_scale=x_plane[:],
+                    start=True,
+                    stop=True,
+                )
+                nc.scalar.activation(y_plain[t][:], y_bank[:], COPY)
+                nc.vector.tensor_scalar(y_unit[t][:], y_plain[t][:], unit_cols[:, t : t + 1], None, MULT)
+
+        w2_grouped = keep.tile([P, N, PACK], BF16, name="w2_grouped", align_bytes=64)
+        w2_codes = keep.tile([P, N], U32, name="w2_codes", align_bytes=64)
+        w2_plane = keep.tile([P, N], U8, name="w2_plane", align_bytes=64)
+
+        def quantize_w2():
+            nc.vector.tensor_copy(
+                w2_grouped[:].rearrange("p (c i) j -> p c j i", i=4),
+                w2_raw[:].rearrange("p j (c i) -> p c j i", i=4),
+            )
+            nc.vector.quantize_mx(
+                out=w2_codes[:].bitcast(FP8X4), scales=w2_plane[:], in_=w2_grouped[:].rearrange("p n j -> p (n j)")
+            )
+
+        starts = [sum(CHUNKS[:k]) for k in range(len(CHUNKS))]
+        products, thirds, hids, hid_codes, hid_planes, banks = {}, {}, {}, {}, {}, {}
+
+        def entries(a_list, k):
+            return a_list[:, starts[k] // LIST_ROWS : (starts[k] + CHUNKS[k]) // LIST_ROWS]
+
+        def gather_second_and_multiply(k, t):
+            second = keep.tile([P, CHUNKS[k]], F32, name=f"second{k}_{t}")
+            nc.scalar.activation(second[:], y_plain[t][:].indirect(entries(gb_list, k)), COPY)
+            nc.vector.tensor_tensor(products[k][:, t, :], y_unit[t][:].indirect(entries(ga_list, k)), second[:], MULT)
+
+        def gather_third(k, t):
+            nc.scalar.activation(thirds[k][:, t, :], y_unit[t][:].indirect(entries(gc_list, k)), COPY)
+
+        def add_and_round(k):
+            hids[k] = keep.tile([P, CHUNKS[k], PACK], BF16, name=f"hid{k}", align_bytes=64)
+            nc.vector.tensor_tensor(
+                hids[k][:].rearrange("p (c i) t -> p c t i", i=4),
+                products[k][:].rearrange("p t (c i) -> p c t i", i=4),
+                thirds[k][:].rearrange("p t (c i) -> p c t i", i=4),
+                ADD,
+            )
+
+        def quantize_and_multiply(k):
+            width = CHUNKS[k]
+            codes = keep.tile([P, width], U32, name=f"hid_codes{k}", align_bytes=64)
+            plane = keep.tile([P, width], U8, name=f"hid_plane{k}", align_bytes=64)
+            nc.vector.quantize_mx(
+                out=codes[:].bitcast(FP8X4), scales=plane[:], in_=hids[k][:].rearrange("p r t -> p (r t)")
+            )
+            banks[k] = psum.tile([P, 2, width], F32, name=f"out_bank{k % 4}")
+            for half in range(2):
+                nc.tensor.matmul_mx(
+                    out=banks[k][:, half, :],
+                    lhsT=w2_codes[:, half * P : (half + 1) * P].bitcast(FP8X4),
+                    lhsT_scale=w2_plane[:, half * P : (half + 1) * P],
+                    rhs=codes[:].bitcast(FP8X4),
+                    rhs_scale=plane[:],
+                    start=True,
+                    stop=True,
+                )
+
+        def store(k):
+            result = keep.tile([P, 2, CHUNKS[k]], F32, name=f"result{k}")
+            nc.vector.tensor_copy(result[:], banks[k][:])
+            nc.sync.dma_start(
+                out.rearrange("(a p) r -> p a r", p=P)[:, :, starts[k] : starts[k] + CHUNKS[k]], result[:]
+            )
+
+        for k in range(len(CHUNKS)):
+            products[k] = keep.tile([P, PACK, CHUNKS[k]], F32, name=f"products{k}")
+            thirds[k] = keep.tile([P, PACK, CHUNKS[k]], F32, name=f"thirds{k}")
+            gather_second_and_multiply(k, 0)
+            if k > 0:
+                add_and_round(k - 1)
+            gather_second_and_multiply(k, 1)
+            if k > 0:
+                quantize_and_multiply(k - 1)
+            gather_second_and_multiply(k, 2)
+            gather_second_and_multiply(k, 3)
+            if k > 0:
+                store(k - 1)
+            else:
+                quantize_w2()
+            for t in range(PACK):
+                gather_third(k, t)
+        last = len(CHUNKS) - 1
+        add_and_round(last)
+        quantize_and_multiply(last)
+        store(last)

@@ -19,7 +19,15 @@ ADD = mybir.AluOpType.add
 P = 128
 PACK = 4
 LIST_ROWS = 16
-CHUNKS = (256, 256, 256, 128, 128)
+PIECE = 512
+SPARE = 16
+FUSED = 256
+CHUNKS = (FUSED,) + (384, 256, 128)
+HID_BUFFER = (0, 0, 0, 0)
+EARLY_STORES = 0
+VECTOR_EMPTIES_Y = (1, 2)
+WALK = 2
+BANK = 512
 
 
 def tile_picked_ytripco_add_p_kernel(tc, x_words, x_scales, w1, unit, w2, offs, ga, gb, gc, out):
@@ -35,97 +43,175 @@ def tile_picked_ytripco_add_p_kernel(tc, x_words, x_scales, w1, unit, w2, offs, 
         gb_list = keep.tile([P, U // LIST_ROWS], U16, name="gb_list")
         gc_list = keep.tile([P, U // LIST_ROWS], U16, name="gc_list")
         w1_raw = [keep.tile([P, PACK, H // 2], F32, name=f"w1_raw{half}") for half in range(2)]
-        w2_raw = keep.tile([P, PACK, N], F32, name="w2_raw")
+        w2_raw = [keep.tile([P, PACK, N // 2], F32, name=f"w2_raw{half}") for half in range(2)]
         unit_cols = keep.tile([P, PACK], F32, name="unit_cols")
+        y_plain = [keep.tile([P, S + SPARE], F32, name=f"y_plain{t}") for t in range(PACK)]
+        y_unit = [keep.tile([P, S + SPARE], F32, name=f"y_unit{t}") for t in range(PACK)]
 
         nc.vector.memset(x_scale_table[:].bitcast(I32), 0)
-        nc.sync.dma_start(x_word_table[:].bitcast(I32), x_words[0].rearrange("p c r -> p (c r)").bitcast(I32))
+        for window in y_plain + y_unit:
+            nc.gpsimd.memset(window[:, S:], 0.0)
+        w1_rows = w1.rearrange("(p j) c -> p j c", j=PACK)
+        w2_rows = w2.rearrange("(p j) n -> p j n", j=PACK)
+        nc.sync.dma_start(w1_raw[0][:], w1_rows[:, :, : H // 2])
         nc.sync.dma_start(offs_list[:], offs)
         for quad in range(4):
-            nc.scalar.dma_start(
+            nc.sync.dma_start(
                 x_scale_table[32 * quad : 32 * quad + 4, :].bitcast(I32),
                 x_scales[0, 4 * quad : 4 * quad + 4, :].bitcast(I32),
             )
-        w1_rows = w1.rearrange("(p j) c -> p j c", j=PACK)
-        for half in range(2):
-            nc.sync.dma_start(w1_raw[half][:], w1_rows[:, :, half * (H // 2) : (half + 1) * (H // 2)])
+        nc.sync.dma_start(w1_raw[1][:], w1_rows[:, :, H // 2 :])
+        nc.sync.dma_start(x_word_table[:].bitcast(I32), x_words[0].rearrange("p c r -> p (c r)").bitcast(I32))
+        nc.sync.dma_start(w2_raw[0][:], w2_rows[:, :, : N // 2])
+        nc.sync.dma_start(w2_raw[1][:], w2_rows[:, :, N // 2 :])
         nc.sync.dma_start(gb_list[:], gb)
         nc.sync.dma_start(unit_cols[:], unit.rearrange("(p t) o -> p (t o)", t=PACK))
         nc.sync.dma_start(ga_list[:], ga)
         nc.sync.dma_start(gc_list[:], gc)
-        nc.sync.dma_start(w2_raw[:], w2.rearrange("(p j) n -> p j n", j=PACK))
 
-        x_codes = keep.tile([P, S], U32, name="x_codes", align_bytes=64)
+        def entries(a_list, start, count):
+            return a_list[:, start // LIST_ROWS : (start + count) // LIST_ROWS]
+
         x_plane = keep.tile([P, S], U8, name="x_plane", align_bytes=64)
-        nc.vector.tensor_copy(x_codes[:], x_word_table[:].indirect(offs_list[:]))
         nc.vector.tensor_copy(x_plane[:], x_scale_table[:].indirect(offs_list[:]))
 
-        y_plain = [keep.tile([P, S], F32, name=f"y_plain{t}") for t in range(PACK)]
-        y_unit = [keep.tile([P, S], F32, name=f"y_unit{t}") for t in range(PACK)]
-        for pair in range(2):
-            grouped = keep.tile([P, 2, P, PACK], BF16, name=f"w1_grouped{pair}", align_bytes=64)
-            for half in range(2):
-                dst = grouped[:, :, half * 64 : (half + 1) * 64, :].rearrange("p t m j -> p m j t")
-                src = w1_raw[half][:].rearrange("p j (m t) -> p m j t", t=PACK)[:, :, :, 2 * pair : 2 * pair + 2]
-                if half == 0:
-                    nc.scalar.activation(dst, src, COPY)
-                else:
-                    nc.vector.tensor_copy(dst, src)
-            codes = keep.tile([P, 2 * P], U32, name=f"w1_codes{pair}", align_bytes=64)
-            plane = keep.tile([P, 2 * P], U8, name=f"w1_plane{pair}", align_bytes=64)
-            nc.vector.quantize_mx(
-                out=codes[:].bitcast(FP8X4), scales=plane[:], in_=grouped[:].rearrange("p t m j -> p (t m j)")
+        w1_grouped = [keep.tile([P, 2, P, PACK], BF16, name=f"w1_grouped{pair}", align_bytes=64) for pair in range(2)]
+        w1_codes = [keep.tile([P, 2 * P], U32, name=f"w1_codes{pair}", align_bytes=64) for pair in range(2)]
+        w1_plane = [keep.tile([P, 2 * P], U8, name=f"w1_plane{pair}", align_bytes=64) for pair in range(2)]
+
+        def w1_views(pair, half):
+            return (
+                w1_grouped[pair][:, :, half * 64 : (half + 1) * 64, :].rearrange("p t m j -> p m j t"),
+                w1_raw[half][:].rearrange("p j (m t) -> p m j t", t=PACK)[:, :, :, 2 * pair : 2 * pair + 2],
             )
-            for slot in range(2):
-                t = 2 * pair + slot
-                y_bank = psum.tile([P, S], F32, name=f"y_bank{t}")
-                nc.tensor.matmul_mx(
-                    out=y_bank[:],
-                    lhsT=codes[:, slot * P : (slot + 1) * P].bitcast(FP8X4),
-                    lhsT_scale=plane[:, slot * P : (slot + 1) * P],
-                    rhs=x_codes[:].bitcast(FP8X4),
-                    rhs_scale=x_plane[:],
-                    start=True,
-                    stop=True,
-                )
-                nc.scalar.activation(y_plain[t][:], y_bank[:], COPY)
-                nc.vector.tensor_scalar(y_unit[t][:], y_plain[t][:], unit_cols[:, t : t + 1], None, MULT)
+
+        def quantize_w1(pair):
+            nc.vector.quantize_mx(
+                out=w1_codes[pair][:].bitcast(FP8X4),
+                scales=w1_plane[pair][:],
+                in_=w1_grouped[pair][:].rearrange("p t m j -> p (t m j)"),
+            )
+
+        nc.scalar.activation(*w1_views(0, 0), COPY)
+        nc.scalar.activation(*w1_views(1, 0), COPY)
+        nc.scalar.activation(*w1_views(0, 1), COPY)
+        nc.scalar.activation(*w1_views(1, 1), COPY)
+        quantize_w1(0)
 
         w2_grouped = keep.tile([P, N, PACK], BF16, name="w2_grouped", align_bytes=64)
         w2_codes = keep.tile([P, N], U32, name="w2_codes", align_bytes=64)
         w2_plane = keep.tile([P, N], U8, name="w2_plane", align_bytes=64)
 
-        def quantize_w2():
-            nc.vector.tensor_copy(
-                w2_grouped[:].rearrange("p (c i) j -> p c j i", i=4),
-                w2_raw[:].rearrange("p j (c i) -> p c j i", i=4),
+        def w2_views(half):
+            dst = w2_grouped[:, half * (N // 2) : (half + 1) * (N // 2), :]
+            return (
+                dst.rearrange("p (c i) j -> p c j i", i=WALK),
+                w2_raw[half][:].rearrange("p j (c i) -> p c j i", i=WALK),
             )
-            nc.vector.quantize_mx(
-                out=w2_codes[:].bitcast(FP8X4), scales=w2_plane[:], in_=w2_grouped[:].rearrange("p n j -> p (n j)")
+
+        nc.scalar.activation(*w2_views(0), COPY)
+
+        x_codes = keep.tile([P, S], U32, name="x_codes", align_bytes=64)
+
+        def first_product(bank, t, start, count):
+            pair, slot = divmod(t, 2)
+            nc.tensor.matmul_mx(
+                out=bank,
+                lhsT=w1_codes[pair][:, slot * P : (slot + 1) * P].bitcast(FP8X4),
+                lhsT_scale=w1_plane[pair][:, slot * P : (slot + 1) * P],
+                rhs=x_codes[:, start : start + count].bitcast(FP8X4),
+                rhs_scale=x_plane[:, start : start + count],
+                start=True,
+                stop=True,
+            )
+
+        for half in range(2):
+            start = half * (S // 2)
+            nc.vector.tensor_copy(
+                x_codes[:, start : start + S // 2], x_word_table[:].indirect(entries(offs_list, start, S // 2))
+            )
+            half_bank = psum.tile([P, S // 2], F32, name=f"bank{half}")
+            first_product(half_bank[:], 0, start, S // 2)
+            nc.scalar.activation(y_plain[0][:, start : start + S // 2], half_bank[:], COPY)
+        quantize_w1(1)
+        y_banks = {}
+        for t in range(1, PACK):
+            y_banks[t] = psum.tile([P, S], F32, name=f"bank{t + 1}")
+            first_product(y_banks[t][:], t, 0, S)
+
+        def empty_y_bank(t):
+            if t in VECTOR_EMPTIES_Y:
+                nc.vector.tensor_copy(y_plain[t][:, :S], y_banks[t][:])
+            else:
+                nc.scalar.activation(y_plain[t][:, :S], y_banks[t][:], COPY)
+
+        def scale_y(t):
+            nc.vector.tensor_scalar(y_unit[t][:, :S], y_plain[t][:, :S], unit_cols[:, t : t + 1], None, MULT)
+
+        products = keep.tile([P, PACK, U], F32, name="products")
+        pieces = U // PIECE
+        seconds = {}
+
+        def gather_second(t, piece):
+            seconds[t, piece] = keep.tile([P, PIECE], F32, name=f"second{t}_{piece}")
+            nc.scalar.activation(
+                seconds[t, piece][:], y_plain[t][:].indirect(entries(gb_list, piece * PIECE, PIECE)), COPY
+            )
+
+        def multiply_by_first(t, piece):
+            nc.vector.tensor_tensor(
+                products[:, t, piece * PIECE : (piece + 1) * PIECE],
+                y_unit[t][:].indirect(entries(ga_list, piece * PIECE, PIECE)),
+                seconds[t, piece][:],
+                MULT,
             )
 
         starts = [sum(CHUNKS[:k]) for k in range(len(CHUNKS))]
-        products, thirds, hids, hid_codes, hid_planes, banks = {}, {}, {}, {}, {}, {}
+        thirds = [keep.tile([P, PACK, width], F32, name=f"thirds{k}") for k, width in enumerate(CHUNKS)]
+        hids, banks = {}, {}
 
-        def entries(a_list, k):
-            return a_list[:, starts[k] // LIST_ROWS : (starts[k] + CHUNKS[k]) // LIST_ROWS]
+        def add_third(t):
+            nc.vector.tensor_tensor(
+                thirds[0][:, t, :], y_unit[t][:].indirect(entries(gc_list, 0, FUSED)), products[:, t, :FUSED], ADD
+            )
 
-        def gather_second_and_multiply(k, t):
-            second = keep.tile([P, CHUNKS[k]], F32, name=f"second{k}_{t}")
-            nc.scalar.activation(second[:], y_plain[t][:].indirect(entries(gb_list, k)), COPY)
-            nc.vector.tensor_tensor(products[k][:, t, :], y_unit[t][:].indirect(entries(ga_list, k)), second[:], MULT)
+        nc.vector.tensor_copy(*w2_views(1))
+        nc.vector.quantize_mx(
+            out=w2_codes[:].bitcast(FP8X4), scales=w2_plane[:], in_=w2_grouped[:].rearrange("p n j -> p (n j)")
+        )
+        scale_y(0)
+        gather_second(0, 0)
+        empty_y_bank(1)
+        scale_y(1)
+        for t in range(PACK):
+            for piece in range(pieces):
+                if (t, piece) != (0, 0):
+                    gather_second(t, piece)
+                multiply_by_first(t, piece)
+            add_third(t)
+            if t + 2 < PACK:
+                empty_y_bank(t + 2)
+                scale_y(t + 2)
 
-        def gather_third(k, t):
-            nc.scalar.activation(thirds[k][:, t, :], y_unit[t][:].indirect(entries(gc_list, k)), COPY)
+        def gather_third(k):
+            for t in range(PACK):
+                nc.scalar.activation(
+                    thirds[k][:, t, :], y_unit[t][:].indirect(entries(gc_list, starts[k], CHUNKS[k])), COPY
+                )
 
         def add_and_round(k):
-            hids[k] = keep.tile([P, CHUNKS[k], PACK], BF16, name=f"hid{k}", align_bytes=64)
-            nc.vector.tensor_tensor(
-                hids[k][:].rearrange("p (c i) t -> p c t i", i=4),
-                products[k][:].rearrange("p t (c i) -> p c t i", i=4),
-                thirds[k][:].rearrange("p t (c i) -> p c t i", i=4),
-                ADD,
-            )
+            start, width = starts[k], CHUNKS[k]
+            hids[k] = keep.tile([P, width, PACK], BF16, name=f"hid{HID_BUFFER[k]}", align_bytes=64)
+            dst = hids[k][:].rearrange("p (c i) t -> p c t i", i=WALK)
+            third = thirds[k][:].rearrange("p t (c i) -> p c t i", i=WALK)
+            if k == 0:
+                nc.vector.tensor_copy(dst, third)
+            else:
+                product = products[:, :, start : start + width].rearrange("p t (c i) -> p c t i", i=WALK)
+                nc.vector.tensor_tensor(dst, product, third, ADD)
+
+        last = len(CHUNKS) - 1
+        bank_names = [f"bank{b}" for b in (5, 6, 7, 0, 1, 2, 3, 4)]
 
         def quantize_and_multiply(k):
             width = CHUNKS[k]
@@ -134,43 +220,50 @@ def tile_picked_ytripco_add_p_kernel(tc, x_words, x_scales, w1, unit, w2, offs, 
             nc.vector.quantize_mx(
                 out=codes[:].bitcast(FP8X4), scales=plane[:], in_=hids[k][:].rearrange("p r t -> p (r t)")
             )
-            banks[k] = psum.tile([P, 2, width], F32, name=f"out_bank{k % 4}")
+            if 2 * width <= BANK and k != last:
+                both = psum.tile([P, 2, width], F32, name=bank_names.pop(0))
+                banks[k] = [both]
+                targets = [both[:, half, :] for half in range(2)]
+            else:
+                banks[k] = [psum.tile([P, 1, width], F32, name=bank_names.pop(0)) for half in range(2)]
+                targets = [bank[:, 0, :] for bank in banks[k]]
+            spans = [(0, width)] if width in (64, 128, 256, 512) else [(0, 256), (256, width)]
             for half in range(2):
-                nc.tensor.matmul_mx(
-                    out=banks[k][:, half, :],
-                    lhsT=w2_codes[:, half * P : (half + 1) * P].bitcast(FP8X4),
-                    lhsT_scale=w2_plane[:, half * P : (half + 1) * P],
-                    rhs=codes[:].bitcast(FP8X4),
-                    rhs_scale=plane[:],
-                    start=True,
-                    stop=True,
-                )
+                for lo, hi in spans:
+                    nc.tensor.matmul_mx(
+                        out=targets[half][:, lo:hi],
+                        lhsT=w2_codes[:, half * P : (half + 1) * P].bitcast(FP8X4),
+                        lhsT_scale=w2_plane[:, half * P : (half + 1) * P],
+                        rhs=codes[:, lo:hi].bitcast(FP8X4),
+                        rhs_scale=plane[:, lo:hi],
+                        start=True,
+                        stop=True,
+                    )
+
+        out_rows = out.rearrange("(a p) r -> p a r", p=P)
 
         def store(k):
+            cols = slice(starts[k], starts[k] + CHUNKS[k])
             result = keep.tile([P, 2, CHUNKS[k]], F32, name=f"result{k}")
-            nc.vector.tensor_copy(result[:], banks[k][:])
-            nc.sync.dma_start(
-                out.rearrange("(a p) r -> p a r", p=P)[:, :, starts[k] : starts[k] + CHUNKS[k]], result[:]
-            )
-
-        for k in range(len(CHUNKS)):
-            products[k] = keep.tile([P, PACK, CHUNKS[k]], F32, name=f"products{k}")
-            thirds[k] = keep.tile([P, PACK, CHUNKS[k]], F32, name=f"thirds{k}")
-            gather_second_and_multiply(k, 0)
-            if k > 0:
-                add_and_round(k - 1)
-            gather_second_and_multiply(k, 1)
-            if k > 0:
-                quantize_and_multiply(k - 1)
-            gather_second_and_multiply(k, 2)
-            gather_second_and_multiply(k, 3)
-            if k > 0:
-                store(k - 1)
+            if len(banks[k]) == 1:
+                nc.scalar.activation(result[:], banks[k][0][:], COPY)
             else:
-                quantize_w2()
-            for t in range(PACK):
-                gather_third(k, t)
-        last = len(CHUNKS) - 1
+                nc.scalar.activation(result[:, 0:1, :], banks[k][0][:], COPY)
+                if k == last:
+                    nc.vector.tensor_copy(result[:, 1:2, :], banks[k][1][:])
+                else:
+                    nc.scalar.activation(result[:, 1:2, :], banks[k][1][:], COPY)
+            nc.sync.dma_start(out_rows[:, :, cols], result[:])
+
+        for k in range(1, last):
+            gather_third(k)
+        for k in range(last):
+            add_and_round(k)
+            quantize_and_multiply(k)
+        for k in range(EARLY_STORES):
+            store(k)
+        gather_third(last)
         add_and_round(last)
         quantize_and_multiply(last)
-        store(last)
+        for k in range(EARLY_STORES, last + 1):
+            store(k)

@@ -21,9 +21,10 @@ PACK = 4
 LIST_ROWS = 16
 PIECE = 512
 SPARE = 16
+WHOLE_LIST_TILES = (2, 3)
 FUSED = 256
 CHUNKS = (FUSED,) + (384, 256, 128)
-HID_BUFFER = (0, 0, 0, 0)
+HID_BUFFER = (0, 1, 2, 3)
 EARLY_STORES = 0
 VECTOR_EMPTIES_Y = (1, 2)
 WALK = 2
@@ -45,12 +46,14 @@ def tile_picked_ytripco_add_p_kernel(tc, x_words, x_scales, w1, unit, w2, offs, 
         w1_raw = [keep.tile([P, PACK, H // 2], F32, name=f"w1_raw{half}") for half in range(2)]
         w2_raw = [keep.tile([P, PACK, N // 2], F32, name=f"w2_raw{half}") for half in range(2)]
         unit_cols = keep.tile([P, PACK], F32, name="unit_cols")
-        y_plain = [keep.tile([P, S + SPARE], F32, name=f"y_plain{t}") for t in range(PACK)]
-        y_unit = [keep.tile([P, S + SPARE], F32, name=f"y_unit{t}") for t in range(PACK)]
+        piece_of = [U if t in WHOLE_LIST_TILES else PIECE for t in range(PACK)]
+        y_plain = [keep.tile([P, piece_of[t] + SPARE], F32, name=f"y_plain{t}") for t in range(PACK)]
+        y_unit = [keep.tile([P, piece_of[t] + SPARE], F32, name=f"y_unit{t}") for t in range(PACK)]
 
         nc.vector.memset(x_scale_table[:].bitcast(I32), 0)
-        for window in y_plain + y_unit:
-            nc.gpsimd.memset(window[:, S:], 0.0)
+        for t in range(PACK):
+            nc.gpsimd.memset(y_plain[t][:, S:], 0.0)
+            nc.gpsimd.memset(y_unit[t][:, S:], 0.0)
         w1_rows = w1.rearrange("(p j) c -> p j c", j=PACK)
         w2_rows = w2.rearrange("(p j) n -> p j n", j=PACK)
         nc.sync.dma_start(w1_raw[0][:], w1_rows[:, :, : H // 2])
@@ -125,18 +128,21 @@ def tile_picked_ytripco_add_p_kernel(tc, x_words, x_scales, w1, unit, w2, offs, 
                 stop=True,
             )
 
+        halves = [slice(half * (S // 2), (half + 1) * (S // 2)) for half in range(2)]
+        half_banks = {}
         for half in range(2):
             start = half * (S // 2)
             nc.vector.tensor_copy(
-                x_codes[:, start : start + S // 2], x_word_table[:].indirect(entries(offs_list, start, S // 2))
+                x_codes[:, halves[half]], x_word_table[:].indirect(entries(offs_list, start, S // 2))
             )
-            half_bank = psum.tile([P, S // 2], F32, name=f"bank{half}")
-            first_product(half_bank[:], 0, start, S // 2)
-            nc.scalar.activation(y_plain[0][:, start : start + S // 2], half_bank[:], COPY)
+            for t in range(2):
+                half_banks[t, half] = psum.tile([P, S // 2], F32, name=f"bank{2 * t + half}")
+                first_product(half_banks[t, half][:], t, start, S // 2)
+            nc.scalar.activation(y_plain[0][:, halves[half]], half_banks[0, half][:], COPY)
         quantize_w1(1)
         y_banks = {}
-        for t in range(1, PACK):
-            y_banks[t] = psum.tile([P, S], F32, name=f"bank{t + 1}")
+        for t in range(2, PACK):
+            y_banks[t] = psum.tile([P, S], F32, name=f"bank{t + 2}")
             first_product(y_banks[t][:], t, 0, S)
 
         def empty_y_bank(t):
@@ -149,20 +155,19 @@ def tile_picked_ytripco_add_p_kernel(tc, x_words, x_scales, w1, unit, w2, offs, 
             nc.vector.tensor_scalar(y_unit[t][:, :S], y_plain[t][:, :S], unit_cols[:, t : t + 1], None, MULT)
 
         products = keep.tile([P, PACK, U], F32, name="products")
-        pieces = U // PIECE
         seconds = {}
 
-        def gather_second(t, piece):
-            seconds[t, piece] = keep.tile([P, PIECE], F32, name=f"second{t}_{piece}")
+        def gather_second(t, start):
+            seconds[t, start] = keep.tile([P, piece_of[t]], F32, name=f"second{t}_{start}")
             nc.scalar.activation(
-                seconds[t, piece][:], y_plain[t][:].indirect(entries(gb_list, piece * PIECE, PIECE)), COPY
+                seconds[t, start][:], y_plain[t][:].indirect(entries(gb_list, start, piece_of[t])), COPY
             )
 
-        def multiply_by_first(t, piece):
+        def multiply_by_first(t, start):
             nc.vector.tensor_tensor(
-                products[:, t, piece * PIECE : (piece + 1) * PIECE],
-                y_unit[t][:].indirect(entries(ga_list, piece * PIECE, PIECE)),
-                seconds[t, piece][:],
+                products[:, t, start : start + piece_of[t]],
+                y_unit[t][:].indirect(entries(ga_list, start, piece_of[t])),
+                seconds[t, start][:],
                 MULT,
             )
 
@@ -179,19 +184,28 @@ def tile_picked_ytripco_add_p_kernel(tc, x_words, x_scales, w1, unit, w2, offs, 
         nc.vector.quantize_mx(
             out=w2_codes[:].bitcast(FP8X4), scales=w2_plane[:], in_=w2_grouped[:].rearrange("p n j -> p (n j)")
         )
-        scale_y(0)
         gather_second(0, 0)
-        empty_y_bank(1)
+        for half in range(2):
+            nc.vector.tensor_copy(y_plain[1][:, halves[half]], half_banks[1, half][:])
+        scale_y(0)
+        empty_y_bank(2)
         scale_y(1)
-        for t in range(PACK):
-            for piece in range(pieces):
-                if (t, piece) != (0, 0):
-                    gather_second(t, piece)
-                multiply_by_first(t, piece)
+        multiply_by_first(0, 0)
+        gather_second(0, PIECE)
+        multiply_by_first(0, PIECE)
+        add_third(0)
+        scale_y(2)
+        for start in (0, PIECE):
+            gather_second(1, start)
+            multiply_by_first(1, start)
+        add_third(1)
+        empty_y_bank(3)
+        nc.scalar.activation(y_unit[3][:, :S], y_banks[3][:], COPY, scale=unit_cols[:, 3:4])
+        for t in (2, 3):
+            gather_second(t, 0)
+            multiply_by_first(t, 0)
+        for t in (2, 3):
             add_third(t)
-            if t + 2 < PACK:
-                empty_y_bank(t + 2)
-                scale_y(t + 2)
 
         def gather_third(k):
             for t in range(PACK):
@@ -211,7 +225,7 @@ def tile_picked_ytripco_add_p_kernel(tc, x_words, x_scales, w1, unit, w2, offs, 
                 nc.vector.tensor_tensor(dst, product, third, ADD)
 
         last = len(CHUNKS) - 1
-        bank_names = [f"bank{b}" for b in (5, 6, 7, 0, 1, 2, 3, 4)]
+        bank_names = [f"bank{b}" for b in (6, 7, 0, 1, 2, 3, 4)]
 
         def quantize_and_multiply(k):
             width = CHUNKS[k]
@@ -220,7 +234,7 @@ def tile_picked_ytripco_add_p_kernel(tc, x_words, x_scales, w1, unit, w2, offs, 
             nc.vector.quantize_mx(
                 out=codes[:].bitcast(FP8X4), scales=plane[:], in_=hids[k][:].rearrange("p r t -> p (r t)")
             )
-            if 2 * width <= BANK and k != last:
+            if k == 0:
                 both = psum.tile([P, 2, width], F32, name=bank_names.pop(0))
                 banks[k] = [both]
                 targets = [both[:, half, :] for half in range(2)]
@@ -247,23 +261,22 @@ def tile_picked_ytripco_add_p_kernel(tc, x_words, x_scales, w1, unit, w2, offs, 
             result = keep.tile([P, 2, CHUNKS[k]], F32, name=f"result{k}")
             if len(banks[k]) == 1:
                 nc.scalar.activation(result[:], banks[k][0][:], COPY)
-            else:
+                nc.sync.dma_start(out_rows[:, :, cols], result[:])
+            elif k > 1:
                 nc.scalar.activation(result[:, 0:1, :], banks[k][0][:], COPY)
-                if k == last:
-                    nc.vector.tensor_copy(result[:, 1:2, :], banks[k][1][:])
-                else:
-                    nc.scalar.activation(result[:, 1:2, :], banks[k][1][:], COPY)
-            nc.sync.dma_start(out_rows[:, :, cols], result[:])
+                nc.vector.tensor_copy(result[:, 1:2, :], banks[k][1][:])
+                nc.sync.dma_start(out_rows[:, :, cols], result[:])
+            else:
+                for half in range(2):
+                    nc.scalar.activation(result[:, half : half + 1, :], banks[k][half][:], COPY)
+                    nc.sync.dma_start(out_rows[:, half : half + 1, cols], result[:, half : half + 1, :])
 
-        for k in range(1, last):
+        for k in range(1, last + 1):
             gather_third(k)
-        for k in range(last):
-            add_and_round(k)
-            quantize_and_multiply(k)
-        for k in range(EARLY_STORES):
-            store(k)
-        gather_third(last)
-        add_and_round(last)
-        quantize_and_multiply(last)
-        for k in range(EARLY_STORES, last + 1):
+        for pair in ((1, 0), (2, 3)):
+            for k in pair:
+                add_and_round(k)
+            for k in pair:
+                quantize_and_multiply(k)
+        for k in (1, 0, 2, 3):
             store(k)

@@ -21,9 +21,9 @@ PACK = 4
 LIST_ROWS = 16
 PIECE = 512
 SPARE = 16
-WHOLE_LIST_TILES = (2, 3)
-FUSED = 256
-CHUNKS = (FUSED,) + (384, 256, 128)
+WHOLE_LIST_TILES = ()
+FUSED = 384
+CHUNKS = (FUSED,) + (256, 256, 128)
 HID_BUFFER = (0, 1, 2, 3)
 EARLY_STORES = 0
 VECTOR_EMPTIES_Y = (1, 2)
@@ -202,9 +202,9 @@ def tile_picked_ytripco_add_p_kernel(tc, x_words, x_scales, w1, unit, w2, offs, 
         empty_y_bank(3)
         nc.scalar.activation(y_unit[3][:, :S], y_banks[3][:], COPY, scale=unit_cols[:, 3:4])
         for t in (2, 3):
-            gather_second(t, 0)
-            multiply_by_first(t, 0)
-        for t in (2, 3):
+            for start in (0, PIECE):
+                gather_second(t, start)
+                multiply_by_first(t, start)
             add_third(t)
 
         def gather_third(k):
@@ -234,7 +234,7 @@ def tile_picked_ytripco_add_p_kernel(tc, x_words, x_scales, w1, unit, w2, offs, 
             nc.vector.quantize_mx(
                 out=codes[:].bitcast(FP8X4), scales=plane[:], in_=hids[k][:].rearrange("p r t -> p (r t)")
             )
-            if k == 0:
+            if k < 2 and 2 * width <= BANK:
                 both = psum.tile([P, 2, width], F32, name=bank_names.pop(0))
                 banks[k] = [both]
                 targets = [both[:, half, :] for half in range(2)]

from contextlib import ExitStack

import concourse.mybir as mybir

K, T, S, N, H, U = 512, 1024, 512, 256, 512, 1024
FLOPS = 2 * K * H * S + 2 * H * N * U

F32 = mybir.dt.float32
BF16 = mybir.dt.bfloat16
I32 = mybir.dt.int32
U32 = mybir.dt.uint32
U16 = mybir.dt.uint16
U8 = mybir.dt.uint8
FP8X4 = mybir.dt.float8_e4m3fn_x4
COPY = mybir.ActivationFunctionType.Copy
MULT = mybir.AluOpType.mult
ADD = mybir.AluOpType.add

P = 128
PACK = 4
LIST_ROWS = 16
PIECE = 512
SPARE = 16
WHOLE_LIST_TILES = ()
FUSED = 384
CHUNKS = (FUSED,) + (256, 256, 128)
HID_BUFFER = (0, 1, 2, 3)
EARLY_STORES = 0
VECTOR_EMPTIES_Y = (1, 2)
WALK = 2
BANK = 512


def tile_picked_ytripco_add_p_kernel(tc, x_words, x_scales, w1, unit, w2, offs, ga, gb, gc, out):
    nc = tc.nc
    with ExitStack() as ctx:
        keep = ctx.enter_context(tc.tile_pool(name="keep", bufs=1))
        psum = ctx.enter_context(tc.psum_pool(name="psum", bufs=1))

        x_word_table = keep.tile([P, T], U32, name="x_word_table")
        x_scale_table = keep.tile([P, T], U8, name="x_scale_table")
        offs_list = keep.tile([P, S // LIST_ROWS], U16, name="offs_list")
        ga_list = keep.tile([P, U // LIST_ROWS], U16, name="ga_list")
        gb_list = keep.tile([P, U // LIST_ROWS], U16, name="gb_list")
        gc_list = keep.tile([P, U // LIST_ROWS], U16, name="gc_list")
        w1_raw = [keep.tile([P, PACK, H // 2], F32, name=f"w1_raw{half}") for half in range(2)]
        w2_raw = [keep.tile([P, PACK, N // 2], F32, name=f"w2_raw{half}") for half in range(2)]
        unit_cols = keep.tile([P, PACK], F32, name="unit_cols")
        piece_of = [U if t in WHOLE_LIST_TILES else PIECE for t in range(PACK)]
        y_plain = [keep.tile([P, piece_of[t] + SPARE], F32, name=f"y_plain{t}") for t in range(PACK)]
        y_unit = [keep.tile([P, piece_of[t] + SPARE], F32, name=f"y_unit{t}") for t in range(PACK)]

        nc.vector.memset(x_scale_table[:].bitcast(I32), 0)
        for t in range(PACK):
            nc.gpsimd.memset(y_plain[t][:, S:], 0.0)
            nc.gpsimd.memset(y_unit[t][:, S:], 0.0)
        w1_rows = w1.rearrange("(p j) c -> p j c", j=PACK)
        w2_rows = w2.rearrange("(p j) n -> p j n", j=PACK)
        nc.sync.dma_start(w1_raw[0][:], w1_rows[:, :, : H // 2])
        nc.sync.dma_start(offs_list[:], offs)
        for quad in range(4):
            nc.sync.dma_start(
                x_scale_table[32 * quad : 32 * quad + 4, :].bitcast(I32),
                x_scales[0, 4 * quad : 4 * quad + 4, :].bitcast(I32),
            )
        nc.sync.dma_start(w1_raw[1][:], w1_rows[:, :, H // 2 :])
        nc.sync.dma_start(x_word_table[:].bitcast(I32), x_words[0].rearrange("p c r -> p (c r)").bitcast(I32))
        nc.sync.dma_start(w2_raw[0][:], w2_rows[:, :, : N // 2])
        nc.sync.dma_start(w2_raw[1][:], w2_rows[:, :, N // 2 :])
        nc.sync.dma_start(gb_list[:], gb)
        nc.sync.dma_start(unit_cols[:], unit.rearrange("(p t) o -> p (t o)", t=PACK))
        nc.sync.dma_start(ga_list[:], ga)
        nc.sync.dma_start(gc_list[:], gc)

        def entries(a_list, start, count):
            return a_list[:, start // LIST_ROWS : (start + count) // LIST_ROWS]

        x_plane = keep.tile([P, S], U8, name="x_plane", align_bytes=64)
        nc.vector.tensor_copy(x_plane[:], x_scale_table[:].indirect(offs_list[:]))

        w1_grouped = [keep.tile([P, 2, P, PACK], BF16, name=f"w1_grouped{pair}", align_bytes=64) for pair in range(2)]
        w1_codes = [keep.tile([P, 2 * P], U32, name=f"w1_codes{pair}", align_bytes=64) for pair in range(2)]
        w1_plane = [keep.tile([P, 2 * P], U8, name=f"w1_plane{pair}", align_bytes=64) for pair in range(2)]

        def w1_views(pair, half):
            return (
                w1_grouped[pair][:, :, half * 64 : (half + 1) * 64, :].rearrange("p t m j -> p m j t"),
                w1_raw[half][:].rearrange("p j (m t) -> p m j t", t=PACK)[:, :, :, 2 * pair : 2 * pair + 2],
            )

        def quantize_w1(pair):
            nc.vector.quantize_mx(
                out=w1_codes[pair][:].bitcast(FP8X4),
                scales=w1_plane[pair][:],
                in_=w1_grouped[pair][:].rearrange("p t m j -> p (t m j)"),
            )

        nc.scalar.activation(*w1_views(0, 0), COPY)
        nc.scalar.activation(*w1_views(1, 0), COPY)
        nc.scalar.activation(*w1_views(0, 1), COPY)
        nc.scalar.activation(*w1_views(1, 1), COPY)
        quantize_w1(0)

        w2_grouped = keep.tile([P, N, PACK], BF16, name="w2_grouped", align_bytes=64)
        w2_codes = keep.tile([P, N], U32, name="w2_codes", align_bytes=64)
        w2_plane = keep.tile([P, N], U8, name="w2_plane", align_bytes=64)

        def w2_views(half):
            dst = w2_grouped[:, half * (N // 2) : (half + 1) * (N // 2), :]
            return (
                dst.rearrange("p (c i) j -> p c j i", i=WALK),
                w2_raw[half][:].rearrange("p j (c i) -> p c j i", i=WALK),
            )

        nc.scalar.activation(*w2_views(0), COPY)

        x_codes = keep.tile([P, S], U32, name="x_codes", align_bytes=64)

        def first_product(bank, t, start, count):
            pair, slot = divmod(t, 2)
            nc.tensor.matmul_mx(
                out=bank,
                lhsT=w1_codes[pair][:, slot * P : (slot + 1) * P].bitcast(FP8X4),
                lhsT_scale=w1_plane[pair][:, slot * P : (slot + 1) * P],
                rhs=x_codes[:, start : start + count].bitcast(FP8X4),
                rhs_scale=x_plane[:, start : start + count],
                start=True,
                stop=True,
            )

        halves = [slice(half * (S // 2), (half + 1) * (S // 2)) for half in range(2)]
        half_banks = {}
        for half in range(2):
            start = half * (S // 2)
            nc.vector.tensor_copy(
                x_codes[:, halves[half]], x_word_table[:].indirect(entries(offs_list, start, S // 2))
            )
            for t in range(2):
                half_banks[t, half] = psum.tile([P, S // 2], F32, name=f"bank{2 * t + half}")
                first_product(half_banks[t, half][:], t, start, S // 2)
            nc.scalar.activation(y_plain[0][:, halves[half]], half_banks[0, half][:], COPY)
        quantize_w1(1)
        y_banks = {}
        for t in range(2, PACK):
            y_banks[t] = psum.tile([P, S], F32, name=f"bank{t + 2}")
            first_product(y_banks[t][:], t, 0, S)

        def empty_y_bank(t):
            if t in VECTOR_EMPTIES_Y:
                nc.vector.tensor_copy(y_plain[t][:, :S], y_banks[t][:])
            else:
                nc.scalar.activation(y_plain[t][:, :S], y_banks[t][:], COPY)

        def scale_y(t):
            nc.vector.tensor_scalar(y_unit[t][:, :S], y_plain[t][:, :S], unit_cols[:, t : t + 1], None, MULT)

        products = keep.tile([P, PACK, U], F32, name="products")
        seconds = {}

        def gather_second(t, start):
            seconds[t, start] = keep.tile([P, piece_of[t]], F32, name=f"second{t}_{start}")
            nc.scalar.activation(
                seconds[t, start][:], y_plain[t][:].indirect(entries(gb_list, start, piece_of[t])), COPY
            )

        def multiply_by_first(t, start):
            nc.vector.tensor_tensor(
                products[:, t, start : start + piece_of[t]],
                y_unit[t][:].indirect(entries(ga_list, start, piece_of[t])),
                seconds[t, start][:],
                MULT,
            )

        starts = [sum(CHUNKS[:k]) for k in range(len(CHUNKS))]
        thirds = [keep.tile([P, PACK, width], F32, name=f"thirds{k}") for k, width in enumerate(CHUNKS)]
        hids, banks = {}, {}

        def add_third(t):
            nc.vector.tensor_tensor(
                thirds[0][:, t, :], y_unit[t][:].indirect(entries(gc_list, 0, FUSED)), products[:, t, :FUSED], ADD
            )

        nc.vector.tensor_copy(*w2_views(1))
        nc.vector.quantize_mx(
            out=w2_codes[:].bitcast(FP8X4), scales=w2_plane[:], in_=w2_grouped[:].rearrange("p n j -> p (n j)")
        )
        gather_second(0, 0)
        for half in range(2):
            nc.vector.tensor_copy(y_plain[1][:, halves[half]], half_banks[1, half][:])
        scale_y(0)
        empty_y_bank(2)
        scale_y(1)
        multiply_by_first(0, 0)
        gather_second(0, PIECE)
        multiply_by_first(0, PIECE)
        add_third(0)
        scale_y(2)
        for start in (0, PIECE):
            gather_second(1, start)
            multiply_by_first(1, start)
        add_third(1)
        empty_y_bank(3)
        nc.scalar.activation(y_unit[3][:, :S], y_banks[3][:], COPY, scale=unit_cols[:, 3:4])
        for t in (2, 3):
            for start in (0, PIECE):
                gather_second(t, start)
                multiply_by_first(t, start)
            add_third(t)

        def gather_third(k):
            for t in range(PACK):
                nc.scalar.activation(
                    thirds[k][:, t, :], y_unit[t][:].indirect(entries(gc_list, starts[k], CHUNKS[k])), COPY
                )

        def add_and_round(k):
            start, width = starts[k], CHUNKS[k]
            hids[k] = keep.tile([P, width, PACK], BF16, name=f"hid{HID_BUFFER[k]}", align_bytes=64)
            dst = hids[k][:].rearrange("p (c i) t -> p c t i", i=WALK)
            third = thirds[k][:].rearrange("p t (c i) -> p c t i", i=WALK)
            if k == 0:
                nc.vector.tensor_copy(dst, third)
            else:
                product = products[:, :, start : start + width].rearrange("p t (c i) -> p c t i", i=WALK)
                nc.vector.tensor_tensor(dst, product, third, ADD)

        last = len(CHUNKS) - 1
        bank_names = [f"bank{b}" for b in (6, 7, 0, 1, 2, 3, 4)]

        def quantize_and_multiply(k):
            width = CHUNKS[k]
            codes = keep.tile([P, width], U32, name=f"hid_codes{k}", align_bytes=64)
            plane = keep.tile([P, width], U8, name=f"hid_plane{k}", align_bytes=64)
            nc.vector.quantize_mx(
                out=codes[:].bitcast(FP8X4), scales=plane[:], in_=hids[k][:].rearrange("p r t -> p (r t)")
            )
            if k < 2 and 2 * width <= BANK:
                both = psum.tile([P, 2, width], F32, name=bank_names.pop(0))
                banks[k] = [both]
                targets = [both[:, half, :] for half in range(2)]
            else:
                banks[k] = [psum.tile([P, 1, width], F32, name=bank_names.pop(0)) for half in range(2)]
                targets = [bank[:, 0, :] for bank in banks[k]]
            spans = [(0, width)] if width in (64, 128, 256, 512) else [(0, 256), (256, width)]
            for half in range(2):
                for lo, hi in spans:
                    nc.tensor.matmul_mx(
                        out=targets[half][:, lo:hi],
                        lhsT=w2_codes[:, half * P : (half + 1) * P].bitcast(FP8X4),
                        lhsT_scale=w2_plane[:, half * P : (half + 1) * P],
                        rhs=codes[:, lo:hi].bitcast(FP8X4),
                        rhs_scale=plane[:, lo:hi],
                        start=True,
                        stop=True,
                    )

        out_rows = out.rearrange("(a p) r -> p a r", p=P)

        def store(k):
            cols = slice(starts[k], starts[k] + CHUNKS[k])
            result = keep.tile([P, 2, CHUNKS[k]], F32, name=f"result{k}")
            if len(banks[k]) == 1:
                nc.scalar.activation(result[:], banks[k][0][:], COPY)
                nc.sync.dma_start(out_rows[:, :, cols], result[:])
            elif k > 1:
                nc.scalar.activation(result[:, 0:1, :], banks[k][0][:], COPY)
                nc.vector.tensor_copy(result[:, 1:2, :], banks[k][1][:])
                nc.sync.dma_start(out_rows[:, :, cols], result[:])
            else:
                for half in range(2):
                    nc.scalar.activation(result[:, half : half + 1, :], banks[k][half][:], COPY)
                    nc.sync.dma_start(out_rows[:, half : half + 1, cols], result[:, half : half + 1, :])

        for k in range(1, last + 1):
            gather_third(k)
        for pair in ((1, 0), (2, 3)):
            for k in pair:
                add_and_round(k)
            for k in pair:
                quantize_and_multiply(k)
        for k in (1, 0, 2, 3):
            store(k)
